import numpy as np
import ml_dtypes


def mxq(x, axis, fmt="e4m3"):
    dtype, down = {"e4m3": (ml_dtypes.float8_e4m3fn, 7), "e5m2": (ml_dtypes.float8_e5m2, 14)}[fmt]
    v = np.moveaxis(np.asarray(x, np.float32).astype(ml_dtypes.bfloat16).astype(np.float64), axis, -1)
    blocks = v.reshape(v.shape[:-1] + (-1, 32))
    amax = np.abs(blocks).max(-1, keepdims=True)
    byte = np.maximum(np.where(amax > 0, np.frexp(amax)[1] - 1 + 127, 0) - down, 1)
    scale = np.exp2(byte - 127.0)
    codes = (blocks / scale).astype(np.float32).astype(dtype).astype(np.float64)
    return np.moveaxis((codes * scale).reshape(v.shape), -1, axis)


WIDE = False


def mx_kscale(k):
    if not WIDE:
        return np.ones(k)
    levels = np.array([30, -30])
    if k % 512:
        return np.exp2(np.random.permutation(np.resize(levels, k // 32))).repeat(32)
    a = np.empty((k // 512, 16))
    for p in range(k // 512):
        a[p, :8] = np.random.permutation(np.resize(levels, 8))
        for g in range(8):
            far = levels[np.abs(levels - a[p, g]) >= 10]
            a[p, g + 8] = far[np.random.randint(len(far))]
    return np.exp2(a.ravel()).repeat(32)


def f64(x):
    return np.asarray(x).astype(np.float64)


def striped(idx):
    return np.tile(np.asarray(idx).reshape(-1, 16).T, (8, 1)).astype(np.uint16)


def unstriped(offs):
    return offs[:16].T.reshape(-1).astype(np.int64)


def striped8(idx):
    return np.asarray(idx).reshape(8, -1, 16).transpose(0, 2, 1).reshape(128, -1).astype(np.uint16)


def unstriped8(offs):
    return offs.reshape(8, 16, -1).transpose(0, 2, 1).reshape(8, -1).astype(np.int64)


def pick8(x, idx, run):
    r = np.arange(len(x))
    return x[r[:, None], idx[r % (8 * run) // run]]


E2M1 = np.array([0.0, 0.5, 1.0, 1.5, 2.0, 3.0, 4.0, 6.0, -0.0, -0.5, -1.0, -1.5, -2.0, -3.0, -4.0, -6.0])


def pack_weight(w, fmt):
    k, n = w.shape
    w = f64(np.asarray(w, np.float32).astype(ml_dtypes.bfloat16)).reshape(k // 32, 32, n)
    amax = np.abs(w).max(1)
    if fmt in ("e4m3", "e5m2"):
        byte = np.frexp(amax)[1] - 1 + 127 - (7 if fmt == "e4m3" else 14)
    else:
        mant, ex = np.frexp(amax / 6.0)
        byte = np.where(mant > 0.5, ex, ex - 1) + 127
    byte = np.clip(np.where(amax > 0, byte, 1), 1, 254)
    scaled = (w * np.exp2(127.0 - byte)[:, None, :]).reshape(k, n).astype(np.float32)
    by_word = np.ascontiguousarray(scaled.reshape(k // 512, 128, 4, n).transpose(0, 1, 3, 2))
    if fmt in ("e4m3", "e5m2"):
        words = by_word.astype(ml_dtypes.float8_e4m3fn if fmt == "e4m3" else ml_dtypes.float8_e5m2).view(np.uint8)
    else:
        c = by_word.astype(ml_dtypes.float4_e2m1fn).view(np.uint8) & 0xF
        words = (c[..., 0::2] | (c[..., 1::2] << 4)).reshape(k // 512, 128, 2 * n)
    return np.ascontiguousarray(words), np.ascontiguousarray(byte.astype(np.uint8).reshape(k // 512, 16, n))


def unpack_weight(words, scales, fmt):
    g, _, n = scales.shape
    words = np.ascontiguousarray(words).reshape(g, 128, n, -1)
    if fmt in ("e4m3", "e5m2"):
        vals = words.view(ml_dtypes.float8_e4m3fn if fmt == "e4m3" else ml_dtypes.float8_e5m2).astype(np.float64)
    else:
        nib = np.empty((g, 128, n, 4), np.uint8)
        nib[..., 0::2] = words & 0xF
        nib[..., 1::2] = words >> 4
        vals = E2M1[nib]
    vals = vals * np.repeat(np.exp2(scales.astype(np.float64) - 127.0), 8, axis=1)[..., None]
    return vals.transpose(0, 1, 3, 2).reshape(g * 512, n)


K, T, J, R, V, C, O, N, E = 512, 1024, 256, 512, 1024, 512, 256, 256, 512


def setup_inputs():
    n = np.random.standard_normal
    idx = np.random.permutation(V)[:R]
    idx2 = np.random.permutation(T)[:J]
    idx3 = np.stack([np.random.permutation(C)[:J] for _ in range(8)])
    idx4 = np.stack([np.random.permutation(C)[:O] for _ in range(8)])
    idx5 = np.random.permutation(E)[:O]
    fk = mx_kscale(K)
    fr = mx_kscale(R)
    xtp = pack_weight(n((K, T)) / fk[:, None], "e4m3")
    wtp = pack_weight(n((K, V)) * 1 / np.sqrt(K) * fk[:, None], "e2m1")
    wbp = pack_weight(n((R, N)) * 1 / np.sqrt(R) / fr[:, None], "e5m2")
    return {
        "xt_words": xtp[0],
        "xt_scales": xtp[1],
        "wt_words": wtp[0],
        "wt_scales": wtp[1],
        "sa": (np.random.uniform(0.5, 1.6, (R, 1)) * fr[:, None]).astype(np.float32),
        "wb_words": wbp[0],
        "wb_scales": wbp[1],
        "so": (np.random.uniform(0.5, 1.6, (N, 1))).astype(np.float32),
        "offs": striped(idx),
        "offs2": striped(idx2),
        "offs3": striped8(idx3),
        "offs4": striped8(idx4),
        "offs5": striped(idx5),
    }


def reference(xt_words, xt_scales, wt_words, wt_scales, sa, wb_words, wb_scales, so, offs, offs2, offs3, offs4, offs5):
    idx = unstriped(offs)
    idx2 = unstriped(offs2)
    idx3 = unstriped8(offs3)
    idx4 = unstriped8(offs4)
    idx5 = unstriped(offs5)
    xtu = unpack_weight(xt_words, xt_scales, "e4m3")
    wtu = unpack_weight(wt_words, wt_scales, "e2m1")
    wbu = unpack_weight(wb_words, wb_scales, "e5m2")
    wtidxg = wtu[:, idx]
    xtidx2g = xtu[:, idx2]
    a = wtidxg.T @ xtidx2g
    pw = np.zeros((R, C))
    pw[np.arange(R)[:, None], idx3[np.arange(R) % 512 // 64]] = a * f64(sa)
    hid = pick8(pw, idx4, 64)
    hidq = mxq(hid, 0, "e4m3")
    p = wbu.T @ hidq
    y = np.zeros((N, E))
    y[:, idx5] = p * f64(so)
    return y

@@ -1,0 +1,138 @@
+from contextlib import ExitStack
+
+import concourse.mybir as mybir
+
+K, T, J, R, V, C, O, N, E = 512, 1024, 256, 512, 1024, 512, 256, 256, 512
+FLOPS = 2 * K * R * J + 2 * R * N * O
+
+F32 = mybir.dt.float32
+BF16 = mybir.dt.bfloat16
+I32 = mybir.dt.int32
+U32 = mybir.dt.uint32
+U16 = mybir.dt.uint16
+U8 = mybir.dt.uint8
+E4M3X4 = mybir.dt.float8_e4m3fn_x4
+E5M2X4 = mybir.dt.float8_e5m2_x4
+E2M1X4 = mybir.dt.float4_e2m1fn_x4
+COPY = mybir.ActivationFunctionType.Copy
+
+P = 128
+PACK = 4
+HALF = 128
+HCOLS = HALF // 16
+
+
+def load_scale_rows(nc, plane, rows):
+    for q in range(4):
+        nc.sync.dma_start(
+            out=plane[32 * q : 32 * q + 4, :].bitcast(I32),
+            in_=rows[0, 4 * q : 4 * q + 4, :].bitcast(I32),
+        )
+
+
+def load_scale_window(nc, plane, rows):
+    for q in range(4):
+        nc.sync.dma_start(
+            out=plane[32 * q : 32 * q + 32, :].bitcast(I32),
+            in_=rows[0, 4 * q : 4 * q + 4, :].bitcast(I32).partition_broadcast(8),
+        )
+
+
+def tile_list_ownstep_kernel(tc, xt_words, xt_scales, wt_words, wt_scales, sa, wb_words, wb_scales, so,
+                                offs, offs2, offs3, offs4, offs5, out):
+    nc = tc.nc
+    with ExitStack() as ctx:
+        keep = ctx.enter_context(tc.tile_pool(name="keep", bufs=1))
+        psum = ctx.enter_context(tc.psum_pool(name="psum", bufs=8))
+
+        wt_plane = keep.tile([P, V], U8, name="wt_plane", align_bytes=64)
+        xt_plane = keep.tile([P, T], U8, name="xt_plane", align_bytes=64)
+        wb_plane = keep.tile([P, N], U8, name="wb_plane", align_bytes=64)
+        nc.vector.memset(wb_plane[:].bitcast(I32), 0)
+
+        list1 = keep.tile([P, R // 16], U16, name="list1")
+        list2 = keep.tile([P, J // 16], U16, name="list2")
+        list3 = keep.tile([P, J // 16], U16, name="list3")
+        list4 = keep.tile([P, O // 16], U16, name="list4")
+        list5 = keep.tile([P, O // 16], U16, name="list5")
+        wt_store = keep.tile([P, V], U16, name="wt_store", align_bytes=64)
+        xt_store = keep.tile([P, T], I32, name="xt_store", align_bytes=64)
+        wb_codes = keep.tile([P, N], I32, name="wb_codes", align_bytes=64)
+        sa_cols = keep.tile([P, PACK], F32, name="sa_cols")
+        so_cols = keep.tile([P, 2], F32, name="so_cols")
+
+        nc.sync.dma_start(list1[:], offs)
+        nc.sync.dma_start(out=wt_store[:].bitcast(I32), in_=wt_words[0].bitcast(I32))
+        load_scale_window(nc, wt_plane, wt_scales)
+        nc.sync.dma_start(list2[:], offs2)
+        nc.sync.dma_start(out=xt_store[:], in_=xt_words[0].rearrange("p n t -> p (n t)").bitcast(I32))
+        load_scale_window(nc, xt_plane, xt_scales)
+        nc.sync.dma_start(list3[:], offs3)
+        nc.sync.dma_start(out=sa_cols[:], in_=sa.rearrange("(p t) o -> p (t o)", t=PACK))
+        nc.sync.dma_start(list4[:], offs4)
+        nc.sync.dma_start(out=wb_codes[:], in_=wb_words[0].rearrange("p n t -> p (n t)").bitcast(I32))
+        load_scale_rows(nc, wb_plane, wb_scales)
+        with nc.allow_non_contiguous_dma(reason="one weight a partition"):
+            nc.sync.dma_start(out=so_cols[:], in_=so.rearrange("(b p) o -> p (b o)", p=P))
+        nc.sync.dma_start(list5[:], offs5)
+
+        boards = [keep.tile([P, C], F32, name="board%d" % t) for t in range(PACK)]
+        for t in range(PACK):
+            nc.vector.memset(boards[t][:], 0.0)
+        pages = [keep.tile([P, E], F32, name="page%d" % b) for b in range(2)]
+        for b in range(2):
+            nc.vector.memset(pages[b][:], 0.0)
+
+        w_picked = keep.tile([P, R], U16, name="w_picked", align_bytes=64)
+        nc.vector.tensor_copy(out=w_picked[:], in_=wt_store[:].indirect(list1[:]))
+        w_scales = keep.tile([P, PACK, P], U8, name="w_scales", align_bytes=64)
+        nc.vector.tensor_copy(out=w_scales[:].rearrange("p t m -> p m t"), in_=wt_plane[:].indirect(list1[:]))
+        by_slot = w_picked[:].rearrange("p (m t) -> p t m", t=PACK)
+        w_first = keep.tile([P, P], U16, name="w_first", align_bytes=64)
+        w_rest = keep.tile([P, PACK - 1, P], U16, name="w_rest", align_bytes=64)
+        nc.vector.tensor_copy(out=w_first[:], in_=by_slot[:, 0, :])
+
+        for h in range(2):
+            part = list2[:, h * HCOLS : (h + 1) * HCOLS]
+            codes = keep.tile([P, HALF], U32, name="x_codes%d" % h, align_bytes=64)
+            scales = keep.tile([P, HALF], U8, name="x_scales%d" % h, align_bytes=64)
+            nc.vector.tensor_copy(out=codes[:], in_=xt_store[:].bitcast(U32).indirect(part))
+            nc.vector.tensor_copy(out=scales[:], in_=xt_plane[:].indirect(part))
+            for t in range(PACK):
+                if h == 0 and t == 1:
+                    nc.vector.tensor_copy(out=w_rest[:], in_=by_slot[:, 1:PACK, :])
+                w_codes = w_first[:] if t == 0 else w_rest[:, t - 1, :]
+                acc = psum.tile([P, HALF], F32, name="acc")
+                nc.tensor.matmul_mx(out=acc[:], lhsT=w_codes.bitcast(E2M1X4), lhsT_scale=w_scales[:, t, :],
+                                    rhs=codes[:].bitcast(E4M3X4), rhs_scale=scales[:], start=True, stop=True)
+                a_sb = keep.tile([P, HALF], F32, name="a%d_%d" % (t, h))
+                if h == 0 and t == 0:
+                    nc.scalar.copy(out=a_sb[:], in_=acc[:])
+                else:
+                    nc.vector.tensor_copy(out=a_sb[:], in_=acc[:])
+                nc.scalar.activation(out=boards[t][:].indirect(list3[:, h * HCOLS : (h + 1) * HCOLS]), in_=a_sb[:],
+                                     func=COPY, scale=sa_cols[:, t : t + 1])
+
+        hids = []
+        for h in range(2):
+            hid = keep.tile([P, PACK * HALF], BF16, name="hid%d" % h, align_bytes=64)
+            for t in range(PACK):
+                nc.scalar.activation(out=hid[:, t : PACK * HALF : PACK],
+                                     in_=boards[t][:].indirect(list4[:, h * HCOLS : (h + 1) * HCOLS]), func=COPY)
+            hids.append(hid)
+
+        for h in range(2):
+            h_codes = keep.tile([P, HALF], U32, name="h_codes%d" % h, align_bytes=64)
+            h_scales = keep.tile([P, HALF], U8, name="h_scales%d" % h, align_bytes=64)
+            nc.vector.quantize_mx(out=h_codes[:].bitcast(E4M3X4), scales=h_scales[:], in_=hids[h][:])
+            for b in range(2):
+                cols = slice(b * P, (b + 1) * P)
+                acc = psum.tile([P, HALF], F32, name="acc")
+                nc.tensor.matmul_mx(out=acc[:], lhsT=wb_codes[:, cols].bitcast(E5M2X4), lhsT_scale=wb_plane[:, cols],
+                                    rhs=h_codes[:].bitcast(E4M3X4), rhs_scale=h_scales[:], start=True, stop=True)
+                p_sb = keep.tile([P, HALF], F32, name="p%d_%d" % (b, h))
+                nc.vector.tensor_copy(out=p_sb[:], in_=acc[:])
+                nc.scalar.activation(out=pages[b][:].indirect(list5[:, h * HCOLS : (h + 1) * HCOLS]), in_=p_sb[:],
+                                     func=COPY, scale=so_cols[:, b : b + 1])
+                if h == 1:
+                    nc.sync.dma_start(out=out[cols, :], in_=pages[b][:])

@@ -20,6 +20,7 @@ P = 128
 PACK = 4
 HALF = 128
 HCOLS = HALF // 16
+HEAD = 2
 
 
 def load_scale_rows(nc, plane, rows):
@@ -30,9 +31,9 @@ def load_scale_rows(nc, plane, rows):
         )
 
 
-def load_scale_window(nc, plane, rows):
+def load_scale_window(queues, plane, rows):
     for q in range(4):
-        nc.sync.dma_start(
+        queues[q % len(queues)].dma_start(
             out=plane[32 * q : 32 * q + 32, :].bitcast(I32),
             in_=rows[0, 4 * q : 4 * q + 4, :].bitcast(I32).partition_broadcast(8),
         )
@@ -62,11 +63,11 @@ def tile_list_ownstep_kernel(tc, xt_words, xt_scales, wt_words, wt_scales, sa, w
         so_cols = keep.tile([P, 2], F32, name="so_cols")
 
         nc.sync.dma_start(list1[:], offs)
+        load_scale_window([nc.scalar, nc.sync], wt_plane, wt_scales)
         nc.sync.dma_start(out=wt_store[:].bitcast(I32), in_=wt_words[0].bitcast(I32))
-        load_scale_window(nc, wt_plane, wt_scales)
         nc.sync.dma_start(list2[:], offs2)
         nc.sync.dma_start(out=xt_store[:], in_=xt_words[0].rearrange("p n t -> p (n t)").bitcast(I32))
-        load_scale_window(nc, xt_plane, xt_scales)
+        load_scale_window([nc.sync], xt_plane, xt_scales)
         nc.sync.dma_start(list3[:], offs3)
         nc.sync.dma_start(out=sa_cols[:], in_=sa.rearrange("(p t) o -> p (t o)", t=PACK))
         nc.sync.dma_start(list4[:], offs4)
@@ -79,52 +80,56 @@ def tile_list_ownstep_kernel(tc, xt_words, xt_scales, wt_words, wt_scales, sa, w
         boards = [keep.tile([P, C], F32, name="board%d" % t) for t in range(PACK)]
         for t in range(PACK):
             nc.vector.memset(boards[t][:], 0.0)
-        pages = [keep.tile([P, E], F32, name="page%d" % b) for b in range(2)]
-        for b in range(2):
-            nc.vector.memset(pages[b][:], 0.0)
 
         w_picked = keep.tile([P, R], U16, name="w_picked", align_bytes=64)
-        nc.vector.tensor_copy(out=w_picked[:], in_=wt_store[:].indirect(list1[:]))
         w_scales = keep.tile([P, PACK, P], U8, name="w_scales", align_bytes=64)
         nc.vector.tensor_copy(out=w_scales[:].rearrange("p t m -> p m t"), in_=wt_plane[:].indirect(list1[:]))
+        nc.vector.tensor_copy(out=w_picked[:], in_=wt_store[:].indirect(list1[:]))
         by_slot = w_picked[:].rearrange("p (m t) -> p t m", t=PACK)
-        w_first = keep.tile([P, P], U16, name="w_first", align_bytes=64)
-        w_rest = keep.tile([P, PACK - 1, P], U16, name="w_rest", align_bytes=64)
-        nc.vector.tensor_copy(out=w_first[:], in_=by_slot[:, 0, :])
+        w_dealt = keep.tile([P, HEAD, P], U16, name="w_head", tag="w_dealt", align_bytes=64)
+        nc.vector.tensor_copy(out=w_dealt[:], in_=by_slot[:, 0:HEAD, :])
 
         for h in range(2):
             part = list2[:, h * HCOLS : (h + 1) * HCOLS]
-            codes = keep.tile([P, HALF], U32, name="x_codes%d" % h, align_bytes=64)
-            scales = keep.tile([P, HALF], U8, name="x_scales%d" % h, align_bytes=64)
+            codes = keep.tile([P, HALF], U32, name="x_codes", align_bytes=64)
+            scales = keep.tile([P, HALF], U8, name="x_scales", align_bytes=64)
             nc.vector.tensor_copy(out=codes[:], in_=xt_store[:].bitcast(U32).indirect(part))
             nc.vector.tensor_copy(out=scales[:], in_=xt_plane[:].indirect(part))
-            for t in range(PACK):
-                if h == 0 and t == 1:
-                    nc.vector.tensor_copy(out=w_rest[:], in_=by_slot[:, 1:PACK, :])
-                w_codes = w_first[:] if t == 0 else w_rest[:, t - 1, :]
-                acc = psum.tile([P, HALF], F32, name="acc")
-                nc.tensor.matmul_mx(out=acc[:], lhsT=w_codes.bitcast(E2M1X4), lhsT_scale=w_scales[:, t, :],
-                                    rhs=codes[:].bitcast(E4M3X4), rhs_scale=scales[:], start=True, stop=True)
-                a_sb = keep.tile([P, HALF], F32, name="a%d_%d" % (t, h))
-                if h == 0 and t == 0:
+            group = 1 if h == 0 else 2
+            for t0 in range(0, PACK, group):
+                if h == 0 and t0 == HEAD:
+                    w_dealt = keep.tile([P, PACK, P], U16, name="w_all", tag="w_dealt", align_bytes=64)
+                    nc.vector.tensor_copy(out=w_dealt[:], in_=by_slot)
+                acc = psum.tile([P, group, HALF], F32, name="acc")
+                for i in range(group):
+                    nc.tensor.matmul_mx(out=acc[:, i, :], lhsT=w_dealt[:, t0 + i, :].bitcast(E2M1X4),
+                                        lhsT_scale=w_scales[:, t0 + i, :],
+                                        rhs=codes[:].bitcast(E4M3X4), rhs_scale=scales[:], start=True, stop=True)
+                a_sb = keep.tile([P, group, HALF], F32, name="a%d_%d" % (t0, h), align_bytes=64)
+                if h == 0 and t0 == 0:
                     nc.scalar.copy(out=a_sb[:], in_=acc[:])
                 else:
                     nc.vector.tensor_copy(out=a_sb[:], in_=acc[:])
-                nc.scalar.activation(out=boards[t][:].indirect(list3[:, h * HCOLS : (h + 1) * HCOLS]), in_=a_sb[:],
-                                     func=COPY, scale=sa_cols[:, t : t + 1])
+                for i in range(group):
+                    t = t0 + i
+                    nc.scalar.activation(out=boards[t][:].indirect(list3[:, h * HCOLS : (h + 1) * HCOLS]),
+                                         in_=a_sb[:, i, :], func=COPY, scale=sa_cols[:, t : t + 1])
 
-        hids = []
+        pages = [keep.tile([P, E], F32, name="page%d" % b, tag=tag, align_bytes=64)
+                 for b, tag in enumerate(("xt_store", "xt_plane"))]
+        for b in range(2):
+            nc.gpsimd.memset(pages[b][:], 0.0)
+
+        hid = keep.tile([P, PACK * O], BF16, name="hid", tag="a0_1", align_bytes=64)
         for h in range(2):
-            hid = keep.tile([P, PACK * HALF], BF16, name="hid%d" % h, align_bytes=64)
             for t in range(PACK):
-                nc.scalar.activation(out=hid[:, t : PACK * HALF : PACK],
+                nc.scalar.activation(out=hid[:, PACK * HALF * h + t : PACK * HALF * (h + 1) : PACK],
                                      in_=boards[t][:].indirect(list4[:, h * HCOLS : (h + 1) * HCOLS]), func=COPY)
-            hids.append(hid)
 
         for h in range(2):
-            h_codes = keep.tile([P, HALF], U32, name="h_codes%d" % h, align_bytes=64)
-            h_scales = keep.tile([P, HALF], U8, name="h_scales%d" % h, align_bytes=64)
-            nc.vector.quantize_mx(out=h_codes[:].bitcast(E4M3X4), scales=h_scales[:], in_=hids[h][:])
+            h_codes = keep.tile([P, HALF], U32, name="h_codes", align_bytes=64)
+            h_scales = keep.tile([P, HALF], U8, name="h_scales", align_bytes=64)
+            nc.vector.quantize_mx(out=h_codes[:].bitcast(E4M3X4), scales=h_scales[:], in_=hid[:, PACK * HALF * h : PACK * HALF * (h + 1)])
             for b in range(2):
                 cols = slice(b * P, (b + 1) * P)
                 acc = psum.tile([P, HALF], F32, name="acc")
@@ -135,4 +140,4 @@ def tile_list_ownstep_kernel(tc, xt_words, xt_scales, wt_words, wt_scales, sa, w
                 nc.scalar.activation(out=pages[b][:].indirect(list5[:, h * HCOLS : (h + 1) * HCOLS]), in_=p_sb[:],
                                      func=COPY, scale=so_cols[:, b : b + 1])
                 if h == 1:
-                    nc.sync.dma_start(out=out[cols, :], in_=pages[b][:])
+                    (nc.sync, nc.scalar)[b].dma_start(out=out[cols, :], in_=pages[b][:])

@@ -81,29 +81,33 @@ def tile_list_ownstep_kernel(tc, xt_words, xt_scales, wt_words, wt_scales, sa, w
         for t in range(PACK):
             nc.vector.memset(boards[t][:], 0.0)
 
+        s_all = keep.tile([P, PACK, P], U8, name="s_all", align_bytes=64)
+        nc.vector.tensor_copy(out=s_all[:].rearrange("p t m -> p m t"), in_=wt_plane[:].indirect(list1[:]))
         w_picked = keep.tile([P, R], U16, name="w_picked", align_bytes=64)
-        w_scales = keep.tile([P, PACK, P], U8, name="w_scales", align_bytes=64)
-        nc.vector.tensor_copy(out=w_scales[:].rearrange("p t m -> p m t"), in_=wt_plane[:].indirect(list1[:]))
         nc.vector.tensor_copy(out=w_picked[:], in_=wt_store[:].indirect(list1[:]))
-        by_slot = w_picked[:].rearrange("p (m t) -> p t m", t=PACK)
-        w_dealt = keep.tile([P, HEAD, P], U16, name="w_head", tag="w_dealt", align_bytes=64)
-        nc.vector.tensor_copy(out=w_dealt[:], in_=by_slot[:, 0:HEAD, :])
+        w_by_slot = w_picked[:].rearrange("p (m t) -> p t m", t=PACK)
+        w_head = [keep.tile([P, P], U16, name="w_head%d" % t, align_bytes=64) for t in range(HEAD)]
+        for t in range(HEAD):
+            nc.vector.tensor_copy(out=w_head[t][:], in_=w_by_slot[:, t, :])
 
         for h in range(2):
             part = list2[:, h * HCOLS : (h + 1) * HCOLS]
-            codes = keep.tile([P, HALF], U32, name="x_codes", align_bytes=64)
-            scales = keep.tile([P, HALF], U8, name="x_scales", align_bytes=64)
+            codes = keep.tile([P, HALF], U32, name="x_codes%d" % h, tag=("x_codes0", "w_head1")[h], align_bytes=64)
+            scales = keep.tile([P, HALF], U8, name="x_scales%d" % h, align_bytes=64)
             nc.vector.tensor_copy(out=codes[:], in_=xt_store[:].bitcast(U32).indirect(part))
             nc.vector.tensor_copy(out=scales[:], in_=xt_plane[:].indirect(part))
             group = 1 if h == 0 else 2
             for t0 in range(0, PACK, group):
                 if h == 0 and t0 == HEAD:
-                    w_dealt = keep.tile([P, PACK, P], U16, name="w_all", tag="w_dealt", align_bytes=64)
-                    nc.vector.tensor_copy(out=w_dealt[:], in_=by_slot)
+                    w_all = keep.tile([P, PACK, P], U16, name="w_all", tag="w_head0", align_bytes=64)
+                    nc.vector.tensor_copy(out=w_all[:], in_=w_by_slot)
                 acc = psum.tile([P, group, HALF], F32, name="acc")
                 for i in range(group):
-                    nc.tensor.matmul_mx(out=acc[:, i, :], lhsT=w_dealt[:, t0 + i, :].bitcast(E2M1X4),
-                                        lhsT_scale=w_scales[:, t0 + i, :],
+                    t = t0 + i
+                    early = h == 0 and t < HEAD
+                    nc.tensor.matmul_mx(out=acc[:, i, :],
+                                        lhsT=(w_head[t][:] if early else w_all[:, t, :]).bitcast(E2M1X4),
+                                        lhsT_scale=s_all[:, t, :],
                                         rhs=codes[:].bitcast(E4M3X4), rhs_scale=scales[:], start=True, stop=True)
                 a_sb = keep.tile([P, group, HALF], F32, name="a%d_%d" % (t0, h), align_bytes=64)
                 if h == 0 and t0 == 0:
@@ -116,9 +120,9 @@ def tile_list_ownstep_kernel(tc, xt_words, xt_scales, wt_words, wt_scales, sa, w
                                          in_=a_sb[:, i, :], func=COPY, scale=sa_cols[:, t : t + 1])
 
         pages = [keep.tile([P, E], F32, name="page%d" % b, tag=tag, align_bytes=64)
-                 for b, tag in enumerate(("xt_store", "xt_plane"))]
+                 for b, tag in enumerate(("w_head0", "w_head1"))]
         for b in range(2):
-            nc.gpsimd.memset(pages[b][:], 0.0)
+            nc.vector.memset(pages[b][:], 0.0)
 
         hid = keep.tile([P, PACK * O], BF16, name="hid", tag="a0_1", align_bytes=64)
         for h in range(2):
@@ -140,4 +144,4 @@ def tile_list_ownstep_kernel(tc, xt_words, xt_scales, wt_words, wt_scales, sa, w
                 nc.scalar.activation(out=pages[b][:].indirect(list5[:, h * HCOLS : (h + 1) * HCOLS]), in_=p_sb[:],
                                      func=COPY, scale=so_cols[:, b : b + 1])
                 if h == 1:
-                    (nc.sync, nc.scalar)[b].dma_start(out=out[cols, :], in_=pages[b][:])
+                    nc.sync.dma_start(out=out[cols, :], in_=pages[b][:])

from contextlib import ExitStack

import concourse.mybir as mybir

K, T, J, R, V, C, O, N, E = 512, 1024, 256, 512, 1024, 512, 256, 256, 512
FLOPS = 2 * K * R * J + 2 * R * N * O

F32 = mybir.dt.float32
BF16 = mybir.dt.bfloat16
I32 = mybir.dt.int32
U32 = mybir.dt.uint32
U16 = mybir.dt.uint16
U8 = mybir.dt.uint8
E4M3X4 = mybir.dt.float8_e4m3fn_x4
E5M2X4 = mybir.dt.float8_e5m2_x4
E2M1X4 = mybir.dt.float4_e2m1fn_x4
COPY = mybir.ActivationFunctionType.Copy

P = 128
PACK = 4
HALF = 128
HCOLS = HALF // 16
HEAD = 2


def load_scale_rows(nc, plane, rows):
    for q in range(4):
        nc.sync.dma_start(
            out=plane[32 * q : 32 * q + 4, :].bitcast(I32),
            in_=rows[0, 4 * q : 4 * q + 4, :].bitcast(I32),
        )


def load_scale_window(queues, plane, rows):
    for q in range(4):
        queues[q % len(queues)].dma_start(
            out=plane[32 * q : 32 * q + 32, :].bitcast(I32),
            in_=rows[0, 4 * q : 4 * q + 4, :].bitcast(I32).partition_broadcast(8),
        )


def tile_list_ownstep_kernel(tc, xt_words, xt_scales, wt_words, wt_scales, sa, wb_words, wb_scales, so,
                                offs, offs2, offs3, offs4, offs5, out):
    nc = tc.nc
    with ExitStack() as ctx:
        keep = ctx.enter_context(tc.tile_pool(name="keep", bufs=1))
        psum = ctx.enter_context(tc.psum_pool(name="psum", bufs=8))

        wt_plane = keep.tile([P, V], U8, name="wt_plane", align_bytes=64)
        xt_plane = keep.tile([P, T], U8, name="xt_plane", align_bytes=64)
        wb_plane = keep.tile([P, N], U8, name="wb_plane", align_bytes=64)
        nc.vector.memset(wb_plane[:].bitcast(I32), 0)

        list1 = keep.tile([P, R // 16], U16, name="list1")
        list2 = keep.tile([P, J // 16], U16, name="list2")
        list3 = keep.tile([P, J // 16], U16, name="list3")
        list4 = keep.tile([P, O // 16], U16, name="list4")
        list5 = keep.tile([P, O // 16], U16, name="list5")
        wt_store = keep.tile([P, V], U16, name="wt_store", align_bytes=64)
        xt_store = keep.tile([P, T], I32, name="xt_store", align_bytes=64)
        wb_codes = keep.tile([P, N], I32, name="wb_codes", align_bytes=64)
        sa_cols = keep.tile([P, PACK], F32, name="sa_cols")
        so_cols = keep.tile([P, 2], F32, name="so_cols")

        nc.sync.dma_start(list1[:], offs)
        load_scale_window([nc.scalar, nc.sync], wt_plane, wt_scales)
        nc.sync.dma_start(out=wt_store[:].bitcast(I32), in_=wt_words[0].bitcast(I32))
        nc.sync.dma_start(list2[:], offs2)
        nc.sync.dma_start(out=xt_store[:], in_=xt_words[0].rearrange("p n t -> p (n t)").bitcast(I32))
        load_scale_window([nc.sync], xt_plane, xt_scales)
        nc.sync.dma_start(list3[:], offs3)
        nc.sync.dma_start(out=sa_cols[:], in_=sa.rearrange("(p t) o -> p (t o)", t=PACK))
        nc.sync.dma_start(list4[:], offs4)
        nc.sync.dma_start(out=wb_codes[:], in_=wb_words[0].rearrange("p n t -> p (n t)").bitcast(I32))
        load_scale_rows(nc, wb_plane, wb_scales)
        with nc.allow_non_contiguous_dma(reason="one weight a partition"):
            nc.sync.dma_start(out=so_cols[:], in_=so.rearrange("(b p) o -> p (b o)", p=P))
        nc.sync.dma_start(list5[:], offs5)

        boards = [keep.tile([P, C], F32, name="board%d" % t) for t in range(PACK)]
        for t in range(PACK):
            nc.vector.memset(boards[t][:], 0.0)

        s_all = keep.tile([P, PACK, P], U8, name="s_all", align_bytes=64)
        nc.vector.tensor_copy(out=s_all[:].rearrange("p t m -> p m t"), in_=wt_plane[:].indirect(list1[:]))
        w_picked = keep.tile([P, R], U16, name="w_picked", align_bytes=64)
        nc.vector.tensor_copy(out=w_picked[:], in_=wt_store[:].indirect(list1[:]))
        w_by_slot = w_picked[:].rearrange("p (m t) -> p t m", t=PACK)
        w_head = [keep.tile([P, P], U16, name="w_head%d" % t, align_bytes=64) for t in range(HEAD)]
        for t in range(HEAD):
            nc.vector.tensor_copy(out=w_head[t][:], in_=w_by_slot[:, t, :])

        for h in range(2):
            part = list2[:, h * HCOLS : (h + 1) * HCOLS]
            codes = keep.tile([P, HALF], U32, name="x_codes%d" % h, tag=("x_codes0", "w_head1")[h], align_bytes=64)
            scales = keep.tile([P, HALF], U8, name="x_scales%d" % h, align_bytes=64)
            nc.vector.tensor_copy(out=codes[:], in_=xt_store[:].bitcast(U32).indirect(part))
            nc.vector.tensor_copy(out=scales[:], in_=xt_plane[:].indirect(part))
            group = 1 if h == 0 else 2
            for t0 in range(0, PACK, group):
                if h == 0 and t0 == HEAD:
                    w_all = keep.tile([P, PACK, P], U16, name="w_all", tag="w_head0", align_bytes=64)
                    nc.vector.tensor_copy(out=w_all[:], in_=w_by_slot)
                acc = psum.tile([P, group, HALF], F32, name="acc")
                for i in range(group):
                    t = t0 + i
                    early = h == 0 and t < HEAD
                    nc.tensor.matmul_mx(out=acc[:, i, :],
                                        lhsT=(w_head[t][:] if early else w_all[:, t, :]).bitcast(E2M1X4),
                                        lhsT_scale=s_all[:, t, :],
                                        rhs=codes[:].bitcast(E4M3X4), rhs_scale=scales[:], start=True, stop=True)
                a_sb = keep.tile([P, group, HALF], F32, name="a%d_%d" % (t0, h), align_bytes=64)
                if h == 0 and t0 == 0:
                    nc.scalar.copy(out=a_sb[:], in_=acc[:])
                else:
                    nc.vector.tensor_copy(out=a_sb[:], in_=acc[:])
                for i in range(group):
                    t = t0 + i
                    nc.scalar.activation(out=boards[t][:].indirect(list3[:, h * HCOLS : (h + 1) * HCOLS]),
                                         in_=a_sb[:, i, :], func=COPY, scale=sa_cols[:, t : t + 1])

        pages = [keep.tile([P, E], F32, name="page%d" % b, tag=tag, align_bytes=64)
                 for b, tag in enumerate(("w_head0", "w_head1"))]
        for b in range(2):
            nc.vector.memset(pages[b][:], 0.0)

        hid = keep.tile([P, PACK * O], BF16, name="hid", tag="a0_1", align_bytes=64)
        for h in range(2):
            for t in range(PACK):
                nc.scalar.activation(out=hid[:, PACK * HALF * h + t : PACK * HALF * (h + 1) : PACK],
                                     in_=boards[t][:].indirect(list4[:, h * HCOLS : (h + 1) * HCOLS]), func=COPY)

        for h in range(2):
            h_codes = keep.tile([P, HALF], U32, name="h_codes", align_bytes=64)
            h_scales = keep.tile([P, HALF], U8, name="h_scales", align_bytes=64)
            nc.vector.quantize_mx(out=h_codes[:].bitcast(E4M3X4), scales=h_scales[:], in_=hid[:, PACK * HALF * h : PACK * HALF * (h + 1)])
            for b in range(2):
                cols = slice(b * P, (b + 1) * P)
                acc = psum.tile([P, HALF], F32, name="acc")
                nc.tensor.matmul_mx(out=acc[:], lhsT=wb_codes[:, cols].bitcast(E5M2X4), lhsT_scale=wb_plane[:, cols],
                                    rhs=h_codes[:].bitcast(E4M3X4), rhs_scale=h_scales[:], start=True, stop=True)
                p_sb = keep.tile([P, HALF], F32, name="p%d_%d" % (b, h))
                nc.vector.tensor_copy(out=p_sb[:], in_=acc[:])
                nc.scalar.activation(out=pages[b][:].indirect(list5[:, h * HCOLS : (h + 1) * HCOLS]), in_=p_sb[:],
                                     func=COPY, scale=so_cols[:, b : b + 1])
                if h == 1:
                    nc.sync.dma_start(out=out[cols, :], in_=pages[b][:])
